import numpy as np
import ml_dtypes


def mxq(x, axis, fmt="e4m3"):
    dtype, down = {"e4m3": (ml_dtypes.float8_e4m3fn, 7), "e5m2": (ml_dtypes.float8_e5m2, 14)}[fmt]
    v = np.moveaxis(np.asarray(x, np.float32).astype(ml_dtypes.bfloat16).astype(np.float64), axis, -1)
    blocks = v.reshape(v.shape[:-1] + (-1, 32))
    amax = np.abs(blocks).max(-1, keepdims=True)
    byte = np.maximum(np.where(amax > 0, np.frexp(amax)[1] - 1 + 127, 0) - down, 1)
    scale = np.exp2(byte - 127.0)
    codes = (blocks / scale).astype(np.float32).astype(dtype).astype(np.float64)
    return np.moveaxis((codes * scale).reshape(v.shape), -1, axis)


WIDE = False


def mx_kscale(k):
    if not WIDE:
        return np.ones(k)
    levels = np.array([30, -30])
    if k % 512:
        return np.exp2(np.random.permutation(np.resize(levels, k // 32))).repeat(32)
    a = np.empty((k // 512, 16))
    for p in range(k // 512):
        a[p, :8] = np.random.permutation(np.resize(levels, 8))
        for g in range(8):
            far = levels[np.abs(levels - a[p, g]) >= 10]
            a[p, g + 8] = far[np.random.randint(len(far))]
    return np.exp2(a.ravel()).repeat(32)


def f64(x):
    return np.asarray(x).astype(np.float64)


def striped(idx):
    return np.tile(np.asarray(idx).reshape(-1, 16).T, (8, 1)).astype(np.uint16)


def unstriped(offs):
    return offs[:16].T.reshape(-1).astype(np.int64)


E2M1 = np.array([0.0, 0.5, 1.0, 1.5, 2.0, 3.0, 4.0, 6.0, -0.0, -0.5, -1.0, -1.5, -2.0, -3.0, -4.0, -6.0])


def pack_weight(w, fmt):
    k, n = w.shape
    w = f64(np.asarray(w, np.float32).astype(ml_dtypes.bfloat16)).reshape(k // 32, 32, n)
    amax = np.abs(w).max(1)
    if fmt in ("e4m3", "e5m2"):
        byte = np.frexp(amax)[1] - 1 + 127 - (7 if fmt == "e4m3" else 14)
    else:
        mant, ex = np.frexp(amax / 6.0)
        byte = np.where(mant > 0.5, ex, ex - 1) + 127
    byte = np.clip(np.where(amax > 0, byte, 1), 1, 254)
    scaled = (w * np.exp2(127.0 - byte)[:, None, :]).reshape(k, n).astype(np.float32)
    by_word = np.ascontiguousarray(scaled.reshape(k // 512, 128, 4, n).transpose(0, 1, 3, 2))
    if fmt in ("e4m3", "e5m2"):
        words = by_word.astype(ml_dtypes.float8_e4m3fn if fmt == "e4m3" else ml_dtypes.float8_e5m2).view(np.uint8)
    else:
        c = by_word.astype(ml_dtypes.float4_e2m1fn).view(np.uint8) & 0xF
        words = (c[..., 0::2] | (c[..., 1::2] << 4)).reshape(k // 512, 128, 2 * n)
    return np.ascontiguousarray(words), np.ascontiguousarray(byte.astype(np.uint8).reshape(k // 512, 16, n))


def unpack_weight(words, scales, fmt):
    g, _, n = scales.shape
    words = np.ascontiguousarray(words).reshape(g, 128, n, -1)
    if fmt in ("e4m3", "e5m2"):
        vals = words.view(ml_dtypes.float8_e4m3fn if fmt == "e4m3" else ml_dtypes.float8_e5m2).astype(np.float64)
    else:
        nib = np.empty((g, 128, n, 4), np.uint8)
        nib[..., 0::2] = words & 0xF
        nib[..., 1::2] = words >> 4
        vals = E2M1[nib]
    vals = vals * np.repeat(np.exp2(scales.astype(np.float64) - 127.0), 8, axis=1)[..., None]
    return vals.transpose(0, 1, 3, 2).reshape(g * 512, n)


def bf(x):
    return np.asarray(x, np.float32).astype(ml_dtypes.bfloat16)


def planes(Y):
    r, m = Y.shape
    b = f64(bf(Y)).reshape(r // 32, 32, m)
    amax = np.abs(b).max(1)
    byte = np.clip(np.where(amax > 0, np.frexp(amax)[1] - 1 + 127 - 7, 1), 1, 254)
    codes = (b * np.exp2(127.0 - byte)[:, None, :]).reshape(r, m).astype(np.float32).astype(ml_dtypes.float8_e4m3fn).view(np.uint8)
    words = codes.reshape(r // 512, 128, 4, m).transpose(0, 1, 3, 2)
    return np.ascontiguousarray(words), np.ascontiguousarray(byte.astype(np.uint8).reshape(r // 512, 16, m))


K, T, J, R, G, N, Z = 512, 1024, 256, 512, 128, 512, 512


def setup_inputs():
    n = np.random.standard_normal
    idx = np.random.permutation(T)[:J]
    idx2 = np.random.permutation(T)[:J]
    idx3 = np.random.permutation(Z)[:G]
    fk = mx_kscale(K)
    fr = mx_kscale(R)
    wp = pack_weight(n((K, R)) * 1 / np.sqrt(K) * fk[:, None] * fr, "e5m2")
    wbp = pack_weight(n((R, N)) * 1 / np.sqrt(R) / fr[:, None], "e2m1")
    return {
        "xf": (n((K, T))).astype(np.float32),
        "fk": (np.random.uniform(0.5, 2.0, (K, 1)) / fk[:, None]).astype(np.float32),
        "w_words": wp[0],
        "w_scales": wp[1],
        "wb_words": wbp[0],
        "wb_scales": wbp[1],
        "tz": (n((N, Z)) * 0.6).astype(np.float32),
        "rw": (np.random.uniform(0.5, 2.0, (1, G))).astype(np.float32),
        "offs": striped(idx),
        "offs2": striped(idx2),
        "offs3": striped(idx3),
    }


def reference(xf, fk, w_words, w_scales, wb_words, wb_scales, tz, rw, offs, offs2, offs3):
    idx = unstriped(offs)
    idx2 = unstriped(offs2)
    idx3 = unstriped(offs3)
    wu = unpack_weight(w_words, w_scales, "e5m2")
    wbu = unpack_weight(wb_words, wb_scales, "e2m1")
    u = (f64(xf)[:, idx] - f64(xf)[:, idx2]) * f64(fk)
    uq = mxq(u, 0, "e5m2")
    a = wu.T @ uq
    hid = a.reshape(R, G, J // G).max(axis=2)
    hidq = mxq(hid, 0, "e5m2")
    p = wbu.T @ hidq
    y = np.maximum(p, f64(tz)[:, idx3]) * f64(rw)
    words, scales = planes(y)
    return y, words, scales

@@ -1,0 +1,180 @@
+from contextlib import ExitStack
+
+import concourse.mybir as mybir
+from concourse.masks import make_identity
+
+K, T, J, R, G, N, Z = 512, 1024, 256, 512, 128, 512, 512
+FLOPS = 2 * K * R * J + 2 * R * N * G
+
+F32 = mybir.dt.float32
+BF16 = mybir.dt.bfloat16
+I32 = mybir.dt.int32
+U32 = mybir.dt.uint32
+U16 = mybir.dt.uint16
+U8 = mybir.dt.uint8
+E5M2X4 = mybir.dt.float8_e5m2_x4
+E4M3X4 = mybir.dt.float8_e4m3fn_x4
+E2M1X4 = mybir.dt.float4_e2m1fn_x4
+ALU = mybir.AluOpType
+COPY = mybir.ActivationFunctionType.Copy
+
+P = 128
+PACK = 4
+HALVES = 2
+JH = J // HALVES
+GH = G // HALVES
+LIST_ROWS = 16
+
+
+def tile_list_pickgaps_pooled_floored_pl_kernel(
+    tc, xf, fk, w_words, w_scales, wb_words, wb_scales, tz, rw, offs, offs2, offs3, out_0, out_1, out_2
+):
+    nc = tc.nc
+    with ExitStack() as ctx:
+        lists = ctx.enter_context(tc.tile_pool(name="lists", bufs=1))
+        sb = ctx.enter_context(tc.tile_pool(name="sb", bufs=1))
+        ps = ctx.enter_context(tc.psum_pool(name="ps", bufs=1))
+
+        def tiles(name, count, shape, dtype):
+            return [sb.tile(shape, dtype, name="%s%d" % (name, i), align_bytes=64) for i in range(count)]
+
+        first = lists.tile([P, J // LIST_ROWS], U16, name="first")
+        second = lists.tile([P, J // LIST_ROWS], U16, name="second")
+        third = lists.tile([P, G // LIST_ROWS], U16, name="third")
+
+        x_rows = tiles("x_rows", PACK, [P, T], F32)
+        tz_rows = tiles("tz_rows", PACK, [P, Z], F32)
+        fk_sb = sb.tile([P, PACK], F32, name="fk_sb")
+        rw_col = sb.tile([P, 1], F32, name="rw_col")
+        w_raw = sb.tile([P, R], I32, name="w_raw", align_bytes=64)
+        wb_raw = sb.tile([P, 2 * N], U8, name="wb_raw", align_bytes=64)
+        ws_raw = sb.tile([P, R], U8, name="ws_raw", align_bytes=64)
+        wbs_raw = sb.tile([P, N], U8, name="wbs_raw", align_bytes=64)
+
+        nc.vector.memset(ws_raw[:].bitcast(I32), 0)
+        nc.vector.memset(wbs_raw[:].bitcast(I32), 0)
+
+        x_view = xf.rearrange("(p t) c -> p t c", t=PACK)
+        tz_view = tz.rearrange("(p t) c -> p t c", t=PACK)
+
+        def load_scale_rows(tile, rows):
+            for q in range(4):
+                nc.sync.dma_start(tile[32 * q : 32 * q + 4, :].bitcast(I32), rows[0, 4 * q : 4 * q + 4, :].bitcast(I32))
+
+        nc.sync.dma_start(second[:], offs2)
+        nc.sync.dma_start(x_rows[0][:], x_view[:, 0, :])
+        nc.sync.dma_start(first[:], offs)
+        nc.sync.dma_start(fk_sb[:], fk.rearrange("(p t) o -> p (t o)", t=PACK))
+        nc.sync.dma_start(x_rows[1][:], x_view[:, 1, :])
+        load_scale_rows(ws_raw, w_scales)
+        nc.sync.dma_start(x_rows[2][:], x_view[:, 2, :])
+        load_scale_rows(wbs_raw, wb_scales)
+        nc.sync.dma_start(x_rows[3][:], x_view[:, 3, :])
+        nc.sync.dma_start(w_raw[:], w_words[0].rearrange("p n t -> p (n t)").bitcast(I32))
+        nc.sync.dma_start(wb_raw[:].bitcast(I32), wb_words[0].bitcast(I32))
+        nc.sync.dma_start(third[:], offs3)
+        with nc.allow_non_contiguous_dma(reason="one weight to a partition"):
+            nc.sync.dma_start(rw_col[:], rw.rearrange("o g -> g o"))
+        for t in range(PACK):
+            nc.sync.dma_start(tz_rows[t][:], tz_view[:, t, :])
+
+        ident = sb.tile([P, P], F32, name="ident")
+        make_identity(nc, ident[:])
+        rw_all = ps.tile([P, G], F32, name="rw_all")
+        nc.tensor.transpose(rw_all[:], rw_col[:].to_broadcast([P, P]), ident[:])
+
+        ws = sb.tile([P, R], U8, name="ws", align_bytes=64)
+        wbs = sb.tile([P, N], U8, name="wbs", align_bytes=64)
+        w_codes = sb.tile([P, R], I32, name="w_codes", align_bytes=64)
+        wb_codes = sb.tile([P, 2 * N], U8, name="wb_codes", align_bytes=64)
+
+        def deal(dst, src):
+            nc.vector.tensor_copy(dst.rearrange("p (t m) -> p t m", t=PACK), src.rearrange("p (m t) -> p t m", t=PACK))
+
+        u_bf = tiles("u_bf", HALVES, [P, JH, PACK], BF16)
+        cols = JH // LIST_ROWS
+        for t in range(PACK):
+            taken = tiles("taken%d_" % t, HALVES, [P, JH], F32)
+            gap = tiles("gap%d_" % t, HALVES, [P, JH], F32)
+            for h in range(HALVES):
+                nc.scalar.activation(taken[h][:], x_rows[t][:].indirect(second[:, h * cols : (h + 1) * cols]), COPY)
+            for h in range(HALVES):
+                nc.vector.tensor_tensor(
+                    gap[h][:], x_rows[t][:].indirect(first[:, h * cols : (h + 1) * cols]), taken[h][:], ALU.subtract
+                )
+            for h in range(HALVES):
+                nc.vector.tensor_scalar(u_bf[h][:, :, t], gap[h][:], fk_sb[:, t : t + 1], None, ALU.mult)
+            if t == 1:
+                deal(ws[:], ws_raw[:])
+            if t == 2:
+                deal(wbs[:], wbs_raw[:])
+
+        u_codes = tiles("u_codes", HALVES, [P, JH], U32)
+        u_scales = tiles("u_scales", HALVES, [P, JH], U8)
+        deal(w_codes[:], w_raw[:])
+        for h in range(HALVES):
+            nc.vector.quantize_mx(u_codes[h][:].bitcast(E5M2X4), u_scales[h][:], u_bf[h][:].rearrange("p j t -> p (j t)"))
+        deal(wb_codes[:].bitcast(U16), wb_raw[:].bitcast(U16))
+
+        hid_bf = sb.tile([P, G, PACK], BF16, name="hid_bf", align_bytes=64)
+        for h in range(HALVES):
+            acc = ps.tile([P, PACK, JH], F32, name="acc%d" % h)
+            for t in range(PACK):
+                nc.tensor.matmul_mx(
+                    acc[:, t, :],
+                    lhsT=w_codes[:, t * P : (t + 1) * P].bitcast(E5M2X4),
+                    lhsT_scale=ws[:, t * P : (t + 1) * P],
+                    rhs=u_codes[h][:].bitcast(E5M2X4),
+                    rhs_scale=u_scales[h][:],
+                    start=True,
+                    stop=True,
+                )
+            nc.vector.tensor_reduce(
+                hid_bf[:, h * GH : (h + 1) * GH, :],
+                acc[:].rearrange("p t (g j) -> p g t j", j=2),
+                mybir.AxisListType.X,
+                ALU.max,
+            )
+
+        hid_codes = sb.tile([P, G], U32, name="hid_codes", align_bytes=64)
+        hid_scales = sb.tile([P, G], U8, name="hid_scales", align_bytes=64)
+        nc.vector.quantize_mx(hid_codes[:].bitcast(E5M2X4), hid_scales[:], hid_bf[:].rearrange("p g t -> p (g t)"))
+
+        floor = tiles("floor", PACK, [P, G], F32)
+        for t in range(PACK):
+            nc.scalar.activation(floor[t][:], tz_rows[t][:].indirect(third[:]), COPY)
+
+        y = sb.tile([P, PACK, G], F32, name="y", align_bytes=64)
+        higher = tiles("higher", PACK, [P, G], F32)
+        out_view = out_0.rearrange("(p t) g -> p t g", t=PACK)
+
+        def weigh(t):
+            nc.vector.tensor_tensor(y[:, t, :], higher[t][:], rw_all[:], ALU.mult)
+            if t % 2 == 1:
+                nc.sync.dma_start(out_view[:, t - 1 : t + 1, :], y[:, t - 1 : t + 1, :])
+
+        for t in range(PACK):
+            prod = ps.tile([P, G], F32, name="prod%d" % t)
+            nc.tensor.matmul_mx(
+                prod[:],
+                lhsT=wb_codes[:, 2 * t * P : 2 * (t + 1) * P].bitcast(E2M1X4),
+                lhsT_scale=wbs[:, t * P : (t + 1) * P],
+                rhs=hid_codes[:].bitcast(E5M2X4),
+                rhs_scale=hid_scales[:],
+                start=True,
+                stop=True,
+            )
+            nc.vector.tensor_tensor(higher[t][:], prod[:], floor[t][:], ALU.max)
+            if t > 0:
+                weigh(t - 1)
+        weigh(PACK - 1)
+
+        y_bf = sb.tile([P, G, PACK], BF16, name="y_bf", align_bytes=64)
+        nc.vector.tensor_copy(y_bf[:], y[:].rearrange("p t g -> p g t"))
+        y_codes = sb.tile([P, G], U32, name="y_codes", align_bytes=64)
+        y_scales = sb.tile([P, G], U8, name="y_scales", align_bytes=64)
+        nc.vector.quantize_mx(y_codes[:].bitcast(E4M3X4), y_scales[:], y_bf[:].rearrange("p g t -> p (g t)"))
+        nc.sync.dma_start(out_1[0].rearrange("p g t -> p (g t)").bitcast(I32), y_codes[:].bitcast(I32))
+        for q in range(4):
+            queue = nc.scalar if q < 2 else nc.sync
+            queue.dma_start(out_2[0, 4 * q : 4 * q + 4, :].bitcast(I32), y_scales[32 * q : 32 * q + 4, :].bitcast(I32))

@@ -43,7 +43,7 @@ def tile_list_pickgaps_pooled_floored_pl_kernel(
         third = lists.tile([P, G // LIST_ROWS], U16, name="third")
 
         x_rows = tiles("x_rows", PACK, [P, T], F32)
-        tz_rows = tiles("tz_rows", PACK, [P, Z], F32)
+        tz_rows = tiles("tz_rows", PACK // 2, [P, 2, Z], F32)
         fk_sb = sb.tile([P, PACK], F32, name="fk_sb")
         rw_col = sb.tile([P, 1], F32, name="rw_col")
         w_raw = sb.tile([P, R], I32, name="w_raw", align_bytes=64)
@@ -51,8 +51,13 @@ def tile_list_pickgaps_pooled_floored_pl_kernel(
         ws_raw = sb.tile([P, R], U8, name="ws_raw", align_bytes=64)
         wbs_raw = sb.tile([P, N], U8, name="wbs_raw", align_bytes=64)
 
-        nc.vector.memset(ws_raw[:].bitcast(I32), 0)
-        nc.vector.memset(wbs_raw[:].bitcast(I32), 0)
+        nc.gpsimd.memset(ws_raw[:].bitcast(I32), 0)
+        nc.gpsimd.memset(wbs_raw[:].bitcast(I32), 0)
+
+        warm_in = sb.tile([P, 1], F32, name="warm_in")
+        warm_out = sb.tile([P, 1], F32, name="warm_out")
+        nc.vector.memset(warm_in[:], 0.0)
+        nc.scalar.activation(warm_out[:], warm_in[:], COPY)
 
         x_view = xf.rearrange("(p t) c -> p t c", t=PACK)
         tz_view = tz.rearrange("(p t) c -> p t c", t=PACK)
@@ -61,22 +66,22 @@ def tile_list_pickgaps_pooled_floored_pl_kernel(
             for q in range(4):
                 nc.sync.dma_start(tile[32 * q : 32 * q + 4, :].bitcast(I32), rows[0, 4 * q : 4 * q + 4, :].bitcast(I32))
 
-        nc.sync.dma_start(second[:], offs2)
         nc.sync.dma_start(x_rows[0][:], x_view[:, 0, :])
+        nc.sync.dma_start(second[:], offs2)
         nc.sync.dma_start(first[:], offs)
         nc.sync.dma_start(fk_sb[:], fk.rearrange("(p t) o -> p (t o)", t=PACK))
         nc.sync.dma_start(x_rows[1][:], x_view[:, 1, :])
         load_scale_rows(ws_raw, w_scales)
         nc.sync.dma_start(x_rows[2][:], x_view[:, 2, :])
-        load_scale_rows(wbs_raw, wb_scales)
         nc.sync.dma_start(x_rows[3][:], x_view[:, 3, :])
         nc.sync.dma_start(w_raw[:], w_words[0].rearrange("p n t -> p (n t)").bitcast(I32))
         nc.sync.dma_start(wb_raw[:].bitcast(I32), wb_words[0].bitcast(I32))
+        load_scale_rows(wbs_raw, wb_scales)
+        nc.sync.dma_start(tz_rows[0][:], tz_view[:, 0:2, :])
         nc.sync.dma_start(third[:], offs3)
         with nc.allow_non_contiguous_dma(reason="one weight to a partition"):
             nc.sync.dma_start(rw_col[:], rw.rearrange("o g -> g o"))
-        for t in range(PACK):
-            nc.sync.dma_start(tz_rows[t][:], tz_view[:, t, :])
+        nc.sync.dma_start(tz_rows[1][:], tz_view[:, 2:4, :])
 
         ident = sb.tile([P, P], F32, name="ident")
         make_identity(nc, ident[:])
@@ -91,30 +96,36 @@ def tile_list_pickgaps_pooled_floored_pl_kernel(
         def deal(dst, src):
             nc.vector.tensor_copy(dst.rearrange("p (t m) -> p t m", t=PACK), src.rearrange("p (m t) -> p t m", t=PACK))
 
+        def deal_slice(dst, src, t):
+            nc.vector.tensor_copy(dst[:, t * P : (t + 1) * P], src.rearrange("p (m t) -> p t m", t=PACK)[:, t, :])
+
         u_bf = tiles("u_bf", HALVES, [P, JH, PACK], BF16)
         cols = JH // LIST_ROWS
         for t in range(PACK):
             taken = tiles("taken%d_" % t, HALVES, [P, JH], F32)
             gap = tiles("gap%d_" % t, HALVES, [P, JH], F32)
+            picks = [x_rows[t][:].indirect(first[:, h * cols : (h + 1) * cols]) for h in range(HALVES)]
             for h in range(HALVES):
                 nc.scalar.activation(taken[h][:], x_rows[t][:].indirect(second[:, h * cols : (h + 1) * cols]), COPY)
+            if t < PACK - 1:
+                picked = sb.tile([P, JH], F32, name="picked%d" % t, align_bytes=64)
+                nc.scalar.activation(picked[:], picks[1], COPY)
+                picks[1] = picked[:]
             for h in range(HALVES):
-                nc.vector.tensor_tensor(
-                    gap[h][:], x_rows[t][:].indirect(first[:, h * cols : (h + 1) * cols]), taken[h][:], ALU.subtract
-                )
+                nc.vector.tensor_tensor(gap[h][:], picks[h], taken[h][:], ALU.subtract)
             for h in range(HALVES):
                 nc.vector.tensor_scalar(u_bf[h][:, :, t], gap[h][:], fk_sb[:, t : t + 1], None, ALU.mult)
             if t == 1:
                 deal(ws[:], ws_raw[:])
-            if t == 2:
-                deal(wbs[:], wbs_raw[:])
 
         u_codes = tiles("u_codes", HALVES, [P, JH], U32)
         u_scales = tiles("u_scales", HALVES, [P, JH], U8)
-        deal(w_codes[:], w_raw[:])
         for h in range(HALVES):
             nc.vector.quantize_mx(u_codes[h][:].bitcast(E5M2X4), u_scales[h][:], u_bf[h][:].rearrange("p j t -> p (j t)"))
+        for t in range(PACK):
+            deal_slice(w_codes[:], w_raw[:], t)
         deal(wb_codes[:].bitcast(U16), wb_raw[:].bitcast(U16))
+        deal(wbs[:], wbs_raw[:])
 
         hid_bf = sb.tile([P, G, PACK], BF16, name="hid_bf", align_bytes=64)
         for h in range(HALVES):
@@ -142,7 +153,7 @@ def tile_list_pickgaps_pooled_floored_pl_kernel(
 
         floor = tiles("floor", PACK, [P, G], F32)
         for t in range(PACK):
-            nc.scalar.activation(floor[t][:], tz_rows[t][:].indirect(third[:]), COPY)
+            nc.scalar.activation(floor[t][:], tz_rows[t // 2][:, t % 2, :].indirect(third[:]), COPY)
 
         y = sb.tile([P, PACK, G], F32, name="y", align_bytes=64)
         higher = tiles("higher", PACK, [P, G], F32)

from contextlib import ExitStack

import concourse.mybir as mybir
from concourse.masks import make_identity

K, T, J, R, G, N, Z = 512, 1024, 256, 512, 128, 512, 512
FLOPS = 2 * K * R * J + 2 * R * N * G

F32 = mybir.dt.float32
BF16 = mybir.dt.bfloat16
I32 = mybir.dt.int32
U32 = mybir.dt.uint32
U16 = mybir.dt.uint16
U8 = mybir.dt.uint8
E5M2X4 = mybir.dt.float8_e5m2_x4
E4M3X4 = mybir.dt.float8_e4m3fn_x4
E2M1X4 = mybir.dt.float4_e2m1fn_x4
ALU = mybir.AluOpType
COPY = mybir.ActivationFunctionType.Copy

P = 128
PACK = 4
HALVES = 2
JH = J // HALVES
GH = G // HALVES
LIST_ROWS = 16


def tile_list_pickgaps_pooled_floored_pl_kernel(
    tc, xf, fk, w_words, w_scales, wb_words, wb_scales, tz, rw, offs, offs2, offs3, out_0, out_1, out_2
):
    nc = tc.nc
    with ExitStack() as ctx:
        lists = ctx.enter_context(tc.tile_pool(name="lists", bufs=1))
        sb = ctx.enter_context(tc.tile_pool(name="sb", bufs=1))
        ps = ctx.enter_context(tc.psum_pool(name="ps", bufs=1))

        def tiles(name, count, shape, dtype):
            return [sb.tile(shape, dtype, name="%s%d" % (name, i), align_bytes=64) for i in range(count)]

        first = lists.tile([P, J // LIST_ROWS], U16, name="first")
        second = lists.tile([P, J // LIST_ROWS], U16, name="second")
        third = lists.tile([P, G // LIST_ROWS], U16, name="third")

        x_rows = tiles("x_rows", PACK, [P, T], F32)
        tz_rows = tiles("tz_rows", PACK // 2, [P, 2, Z], F32)
        fk_sb = sb.tile([P, PACK], F32, name="fk_sb")
        rw_col = sb.tile([P, 1], F32, name="rw_col")
        w_raw = sb.tile([P, R], I32, name="w_raw", align_bytes=64)
        wb_raw = sb.tile([P, 2 * N], U8, name="wb_raw", align_bytes=64)
        ws_raw = sb.tile([P, R], U8, name="ws_raw", align_bytes=64)
        wbs_raw = sb.tile([P, N], U8, name="wbs_raw", align_bytes=64)

        nc.gpsimd.memset(ws_raw[:].bitcast(I32), 0)
        nc.gpsimd.memset(wbs_raw[:].bitcast(I32), 0)

        warm_in = sb.tile([P, 1], F32, name="warm_in")
        warm_out = sb.tile([P, 1], F32, name="warm_out")
        nc.vector.memset(warm_in[:], 0.0)
        nc.scalar.activation(warm_out[:], warm_in[:], COPY)

        x_view = xf.rearrange("(p t) c -> p t c", t=PACK)
        tz_view = tz.rearrange("(p t) c -> p t c", t=PACK)

        def load_scale_rows(tile, rows):
            for q in range(4):
                nc.sync.dma_start(tile[32 * q : 32 * q + 4, :].bitcast(I32), rows[0, 4 * q : 4 * q + 4, :].bitcast(I32))

        nc.sync.dma_start(x_rows[0][:], x_view[:, 0, :])
        nc.sync.dma_start(second[:], offs2)
        nc.sync.dma_start(first[:], offs)
        nc.sync.dma_start(fk_sb[:], fk.rearrange("(p t) o -> p (t o)", t=PACK))
        nc.sync.dma_start(x_rows[1][:], x_view[:, 1, :])
        load_scale_rows(ws_raw, w_scales)
        nc.sync.dma_start(x_rows[2][:], x_view[:, 2, :])
        nc.sync.dma_start(x_rows[3][:], x_view[:, 3, :])
        nc.sync.dma_start(w_raw[:], w_words[0].rearrange("p n t -> p (n t)").bitcast(I32))
        nc.sync.dma_start(wb_raw[:].bitcast(I32), wb_words[0].bitcast(I32))
        load_scale_rows(wbs_raw, wb_scales)
        nc.sync.dma_start(tz_rows[0][:], tz_view[:, 0:2, :])
        nc.sync.dma_start(third[:], offs3)
        with nc.allow_non_contiguous_dma(reason="one weight to a partition"):
            nc.sync.dma_start(rw_col[:], rw.rearrange("o g -> g o"))
        nc.sync.dma_start(tz_rows[1][:], tz_view[:, 2:4, :])

        ident = sb.tile([P, P], F32, name="ident")
        make_identity(nc, ident[:])
        rw_all = ps.tile([P, G], F32, name="rw_all")
        nc.tensor.transpose(rw_all[:], rw_col[:].to_broadcast([P, P]), ident[:])

        ws = sb.tile([P, R], U8, name="ws", align_bytes=64)
        wbs = sb.tile([P, N], U8, name="wbs", align_bytes=64)
        w_codes = sb.tile([P, R], I32, name="w_codes", align_bytes=64)
        wb_codes = sb.tile([P, 2 * N], U8, name="wb_codes", align_bytes=64)

        def deal(dst, src):
            nc.vector.tensor_copy(dst.rearrange("p (t m) -> p t m", t=PACK), src.rearrange("p (m t) -> p t m", t=PACK))

        def deal_slice(dst, src, t):
            nc.vector.tensor_copy(dst[:, t * P : (t + 1) * P], src.rearrange("p (m t) -> p t m", t=PACK)[:, t, :])

        u_bf = tiles("u_bf", HALVES, [P, JH, PACK], BF16)
        cols = JH // LIST_ROWS
        for t in range(PACK):
            taken = tiles("taken%d_" % t, HALVES, [P, JH], F32)
            gap = tiles("gap%d_" % t, HALVES, [P, JH], F32)
            picks = [x_rows[t][:].indirect(first[:, h * cols : (h + 1) * cols]) for h in range(HALVES)]
            for h in range(HALVES):
                nc.scalar.activation(taken[h][:], x_rows[t][:].indirect(second[:, h * cols : (h + 1) * cols]), COPY)
            if t < PACK - 1:
                picked = sb.tile([P, JH], F32, name="picked%d" % t, align_bytes=64)
                nc.scalar.activation(picked[:], picks[1], COPY)
                picks[1] = picked[:]
            for h in range(HALVES):
                nc.vector.tensor_tensor(gap[h][:], picks[h], taken[h][:], ALU.subtract)
            for h in range(HALVES):
                nc.vector.tensor_scalar(u_bf[h][:, :, t], gap[h][:], fk_sb[:, t : t + 1], None, ALU.mult)
            if t == 1:
                deal(ws[:], ws_raw[:])

        u_codes = tiles("u_codes", HALVES, [P, JH], U32)
        u_scales = tiles("u_scales", HALVES, [P, JH], U8)
        for h in range(HALVES):
            nc.vector.quantize_mx(u_codes[h][:].bitcast(E5M2X4), u_scales[h][:], u_bf[h][:].rearrange("p j t -> p (j t)"))
        for t in range(PACK):
            deal_slice(w_codes[:], w_raw[:], t)
        deal(wb_codes[:].bitcast(U16), wb_raw[:].bitcast(U16))
        deal(wbs[:], wbs_raw[:])

        hid_bf = sb.tile([P, G, PACK], BF16, name="hid_bf", align_bytes=64)
        for h in range(HALVES):
            acc = ps.tile([P, PACK, JH], F32, name="acc%d" % h)
            for t in range(PACK):
                nc.tensor.matmul_mx(
                    acc[:, t, :],
                    lhsT=w_codes[:, t * P : (t + 1) * P].bitcast(E5M2X4),
                    lhsT_scale=ws[:, t * P : (t + 1) * P],
                    rhs=u_codes[h][:].bitcast(E5M2X4),
                    rhs_scale=u_scales[h][:],
                    start=True,
                    stop=True,
                )
            nc.vector.tensor_reduce(
                hid_bf[:, h * GH : (h + 1) * GH, :],
                acc[:].rearrange("p t (g j) -> p g t j", j=2),
                mybir.AxisListType.X,
                ALU.max,
            )

        hid_codes = sb.tile([P, G], U32, name="hid_codes", align_bytes=64)
        hid_scales = sb.tile([P, G], U8, name="hid_scales", align_bytes=64)
        nc.vector.quantize_mx(hid_codes[:].bitcast(E5M2X4), hid_scales[:], hid_bf[:].rearrange("p g t -> p (g t)"))

        floor = tiles("floor", PACK, [P, G], F32)
        for t in range(PACK):
            nc.scalar.activation(floor[t][:], tz_rows[t // 2][:, t % 2, :].indirect(third[:]), COPY)

        y = sb.tile([P, PACK, G], F32, name="y", align_bytes=64)
        higher = tiles("higher", PACK, [P, G], F32)
        out_view = out_0.rearrange("(p t) g -> p t g", t=PACK)

        def weigh(t):
            nc.vector.tensor_tensor(y[:, t, :], higher[t][:], rw_all[:], ALU.mult)
            if t % 2 == 1:
                nc.sync.dma_start(out_view[:, t - 1 : t + 1, :], y[:, t - 1 : t + 1, :])

        for t in range(PACK):
            prod = ps.tile([P, G], F32, name="prod%d" % t)
            nc.tensor.matmul_mx(
                prod[:],
                lhsT=wb_codes[:, 2 * t * P : 2 * (t + 1) * P].bitcast(E2M1X4),
                lhsT_scale=wbs[:, t * P : (t + 1) * P],
                rhs=hid_codes[:].bitcast(E5M2X4),
                rhs_scale=hid_scales[:],
                start=True,
                stop=True,
            )
            nc.vector.tensor_tensor(higher[t][:], prod[:], floor[t][:], ALU.max)
            if t > 0:
                weigh(t - 1)
        weigh(PACK - 1)

        y_bf = sb.tile([P, G, PACK], BF16, name="y_bf", align_bytes=64)
        nc.vector.tensor_copy(y_bf[:], y[:].rearrange("p t g -> p g t"))
        y_codes = sb.tile([P, G], U32, name="y_codes", align_bytes=64)
        y_scales = sb.tile([P, G], U8, name="y_scales", align_bytes=64)
        nc.vector.quantize_mx(y_codes[:].bitcast(E4M3X4), y_scales[:], y_bf[:].rearrange("p g t -> p (g t)"))
        nc.sync.dma_start(out_1[0].rearrange("p g t -> p (g t)").bitcast(I32), y_codes[:].bitcast(I32))
        for q in range(4):
            queue = nc.scalar if q < 2 else nc.sync
            queue.dma_start(out_2[0, 4 * q : 4 * q + 4, :].bitcast(I32), y_scales[32 * q : 32 * q + 4, :].bitcast(I32))
